import numpy as np
import ml_dtypes

BF16 = ml_dtypes.bfloat16


def bf(x):
    return np.asarray(x, np.float32).astype(BF16)


def f32(x):
    return np.asarray(x, np.float32)


def f64(x):
    return np.asarray(x).astype(np.float64)


def striped(idx):
    return np.tile(idx.reshape(-1, 16).T, (8, 1))


S, K, M, N = 512, 128, 512, 384


def setup_inputs():
    return {"base": bf(np.random.standard_normal((M, S))), "x": bf(np.random.standard_normal((K, N))), "w": bf(np.random.standard_normal((K, M)) / np.sqrt(K)), "c": f32(0.2 + 0.8 * np.random.random_sample((1, S))), "offs": striped(np.random.permutation(S)[:N])}


def reference(base, x, w, c, offs):
    idx = offs[:16].T.reshape(-1)
    z = f64(base).copy()
    z[:, idx] = f64(w).T @ f64(x)
    return z * f64(c)

@@ -1,0 +1,62 @@
+import concourse.mybir as mybir
+from concourse.masks import make_identity
+
+BF16, F32, U16 = mybir.dt.bfloat16, mybir.dt.float32, mybir.dt.uint16
+
+P = 128
+S = 512
+M = 512
+N = 384
+BLOCKS = M // P
+
+FLOPS = 2 * P * M * N
+BYTES = P * N * 2 + P * M * 2 + S * 4 + P * (N // 16) * 2 + M * (S - N) * 2 + M * S * 4
+
+
+def tile_scatter_matmul_kernel(tc, base, x, w, c, offs, out):
+    nc = tc.nc
+    with (
+        tc.tile_pool(name="held", bufs=1) as held,
+        tc.psum_pool(name="banks", bufs=1) as banks,
+    ):
+        offsets = held.tile([P, N // 16], U16, name="offsets")
+        nc.sync.dma_start(offsets[:], offs)
+
+        ident = held.tile([P, P], BF16, name="ident")
+        make_identity(nc, ident[:])
+
+        base_blocks = []
+        for b in range(BLOCKS):
+            base_block = held.tile([P, S], BF16, name=f"base{b}")
+            queue = nc.sync if b % 2 == 0 else nc.scalar
+            queue.dma_start(base_block[:], base[b * P : (b + 1) * P, :])
+            base_blocks.append(base_block)
+
+        x_tile = held.tile([P, N], BF16, name="x_tile")
+        nc.sync.dma_start(x_tile[:], x)
+        w_tile = held.tile([P, M], BF16, name="w_tile")
+        nc.scalar.dma_start(w_tile[:], w)
+
+        c_rows = held.tile([P, S], F32, name="c_rows")
+        nc.gpsimd.dma_start(c_rows[:], c.partition_broadcast(P))
+
+        windows = []
+        for b in range(BLOCKS):
+            window = banks.tile([P, S], F32, name=f"window{b}")
+            nc.tensor.matmul(window[:], ident[:], base_blocks[b][:], start=True, stop=True)
+            windows.append(window)
+
+        for b in range(BLOCKS):
+            nc.tensor.matmul(
+                windows[b][:].indirect(offsets[:]),
+                w_tile[:, b * P : (b + 1) * P],
+                x_tile[:],
+                start=True,
+                stop=True,
+            )
+
+        for b in range(BLOCKS):
+            scaled = held.tile([P, S], F32, name=f"scaled{b}")
+            nc.vector.tensor_tensor(scaled[:], windows[b][:], c_rows[:], mybir.AluOpType.mult)
+            queue = nc.sync if b % 2 == 0 else nc.scalar
+            queue.dma_start(out[b * P : (b + 1) * P, :], scaled[:])

@@ -8,6 +8,8 @@ S = 512
 M = 512
 N = 384
 BLOCKS = M // P
+WARM_COLUMNS = 256
+WARM_MATMULS = 6
 
 FLOPS = 2 * P * M * N
 BYTES = P * N * 2 + P * M * 2 + S * 4 + P * (N // 16) * 2 + M * (S - N) * 2 + M * S * 4
@@ -19,26 +21,29 @@ def tile_scatter_matmul_kernel(tc, base, x, w, c, offs, out):
         tc.tile_pool(name="held", bufs=1) as held,
         tc.psum_pool(name="banks", bufs=1) as banks,
     ):
-        offsets = held.tile([P, N // 16], U16, name="offsets")
-        nc.sync.dma_start(offsets[:], offs)
-
-        ident = held.tile([P, P], BF16, name="ident")
-        make_identity(nc, ident[:])
-
         base_blocks = []
         for b in range(BLOCKS):
             base_block = held.tile([P, S], BF16, name=f"base{b}")
             queue = nc.sync if b % 2 == 0 else nc.scalar
             queue.dma_start(base_block[:], base[b * P : (b + 1) * P, :])
             base_blocks.append(base_block)
-
+        offsets = held.tile([P, N // 16], U16, name="offsets")
+        nc.sync.dma_start(offsets[:], offs)
         x_tile = held.tile([P, N], BF16, name="x_tile")
         nc.sync.dma_start(x_tile[:], x)
         w_tile = held.tile([P, M], BF16, name="w_tile")
         nc.scalar.dma_start(w_tile[:], w)
-
         c_rows = held.tile([P, S], F32, name="c_rows")
-        nc.gpsimd.dma_start(c_rows[:], c.partition_broadcast(P))
+        nc.scalar.dma_start(c_rows[:], c.partition_broadcast(P))
+
+        ident = held.tile([P, P], BF16, name="ident")
+        make_identity(nc, ident[:])
+
+        zeros = held.tile([P, WARM_COLUMNS], BF16, name="zeros")
+        nc.vector.memset(zeros[:], 0.0)
+        unread = banks.tile([P, WARM_COLUMNS], F32, name="unread")
+        for i in range(WARM_MATMULS):
+            nc.tensor.matmul(unread[:], zeros[:, 0:P], zeros[:], start=True, stop=True)
 
         windows = []
         for b in range(BLOCKS):

@@ -8,8 +8,6 @@ S = 512
 M = 512
 N = 384
 BLOCKS = M // P
-WARM_COLUMNS = 256
-WARM_MATMULS = 6
 
 FLOPS = 2 * P * M * N
 BYTES = P * N * 2 + P * M * 2 + S * 4 + P * (N // 16) * 2 + M * (S - N) * 2 + M * S * 4
@@ -21,29 +19,23 @@ def tile_scatter_matmul_kernel(tc, base, x, w, c, offs, out):
         tc.tile_pool(name="held", bufs=1) as held,
         tc.psum_pool(name="banks", bufs=1) as banks,
     ):
+        c_rows = held.tile([P, S], F32, name="c_rows")
+        nc.scalar.dma_start(c_rows[:], c.partition_broadcast(P))
+        x_tile = held.tile([P, N], BF16, name="x_tile")
+        nc.scalar.dma_start(x_tile[:], x)
+        w_tile = held.tile([P, M], BF16, name="w_tile")
+        nc.scalar.dma_start(w_tile[:], w)
+
         base_blocks = []
         for b in range(BLOCKS):
             base_block = held.tile([P, S], BF16, name=f"base{b}")
-            queue = nc.sync if b % 2 == 0 else nc.scalar
-            queue.dma_start(base_block[:], base[b * P : (b + 1) * P, :])
+            nc.sync.dma_start(base_block[:], base[b * P : (b + 1) * P, :])
             base_blocks.append(base_block)
         offsets = held.tile([P, N // 16], U16, name="offsets")
         nc.sync.dma_start(offsets[:], offs)
-        x_tile = held.tile([P, N], BF16, name="x_tile")
-        nc.sync.dma_start(x_tile[:], x)
-        w_tile = held.tile([P, M], BF16, name="w_tile")
-        nc.scalar.dma_start(w_tile[:], w)
-        c_rows = held.tile([P, S], F32, name="c_rows")
-        nc.scalar.dma_start(c_rows[:], c.partition_broadcast(P))
 
         ident = held.tile([P, P], BF16, name="ident")
         make_identity(nc, ident[:])
-
-        zeros = held.tile([P, WARM_COLUMNS], BF16, name="zeros")
-        nc.vector.memset(zeros[:], 0.0)
-        unread = banks.tile([P, WARM_COLUMNS], F32, name="unread")
-        for i in range(WARM_MATMULS):
-            nc.tensor.matmul(unread[:], zeros[:, 0:P], zeros[:], start=True, stop=True)
 
         windows = []
         for b in range(BLOCKS):

@@ -8,6 +8,7 @@ S = 512
 M = 512
 N = 384
 BLOCKS = M // P
+WARM_MATMULS = 3
 
 FLOPS = 2 * P * M * N
 BYTES = P * N * 2 + P * M * 2 + S * 4 + P * (N // 16) * 2 + M * (S - N) * 2 + M * S * 4
@@ -20,22 +21,31 @@ def tile_scatter_matmul_kernel(tc, base, x, w, c, offs, out):
         tc.psum_pool(name="banks", bufs=1) as banks,
     ):
         c_rows = held.tile([P, S], F32, name="c_rows")
-        nc.scalar.dma_start(c_rows[:], c.partition_broadcast(P))
-        x_tile = held.tile([P, N], BF16, name="x_tile")
-        nc.scalar.dma_start(x_tile[:], x)
-        w_tile = held.tile([P, M], BF16, name="w_tile")
-        nc.scalar.dma_start(w_tile[:], w)
+        nc.gpsimd.dma_start(c_rows[:], c.partition_broadcast(P))
+
+        offsets = held.tile([P, N // 16], U16, name="offsets")
+        nc.sync.dma_start(offsets[:], offs)
 
         base_blocks = []
         for b in range(BLOCKS):
             base_block = held.tile([P, S], BF16, name=f"base{b}")
-            nc.sync.dma_start(base_block[:], base[b * P : (b + 1) * P, :])
+            queue = nc.sync if b % 2 == 0 else nc.scalar
+            queue.dma_start(base_block[:], base[b * P : (b + 1) * P, :])
             base_blocks.append(base_block)
-        offsets = held.tile([P, N // 16], U16, name="offsets")
-        nc.sync.dma_start(offsets[:], offs)
+        x_tile = held.tile([P, N], BF16, name="x_tile")
+        nc.sync.dma_start(x_tile[:], x)
+        w_tile = held.tile([P, M], BF16, name="w_tile")
+        nc.scalar.dma_start(w_tile[:], w)
+
+        zeros = held.tile([P, S], BF16, name="zeros")
+        nc.vector.memset(zeros[:], 0.0)
+        unread = banks.tile([P, S], F32, name="unread")
+        for i in range(WARM_MATMULS):
+            nc.tensor.matmul(unread[:], zeros[:, 0:P], zeros[:], start=True, stop=True)
 
         ident = held.tile([P, P], BF16, name="ident")
-        make_identity(nc, ident[:])
+        nc.vector.memset(ident[:], 0.0)
+        make_identity(nc, ident[:], nomemset=True)
 
         windows = []
         for b in range(BLOCKS):

@@ -20,8 +20,8 @@ def tile_scatter_matmul_kernel(tc, base, x, w, c, offs, out):
         tc.tile_pool(name="held", bufs=1) as held,
         tc.psum_pool(name="banks", bufs=1) as banks,
     ):
-        c_rows = held.tile([P, S], F32, name="c_rows")
-        nc.gpsimd.dma_start(c_rows[:], c.partition_broadcast(P))
+        c_row = held.tile([1, S], F32, name="c_row")
+        nc.scalar.dma_start(c_row[:], c)
 
         offsets = held.tile([P, N // 16], U16, name="offsets")
         nc.sync.dma_start(offsets[:], offs)
@@ -46,6 +46,13 @@ def tile_scatter_matmul_kernel(tc, base, x, w, c, offs, out):
         ident = held.tile([P, P], BF16, name="ident")
         nc.vector.memset(ident[:], 0.0)
         make_identity(nc, ident[:], nomemset=True)
+
+        ones = held.tile([1, P], F32, name="ones")
+        nc.vector.memset(ones[:], 1.0)
+        c_bank = banks.tile([P, S], F32, name="c_bank")
+        nc.tensor.matmul(c_bank[:], ones[:], c_row[:], start=True, stop=True)
+        c_rows = held.tile([P, S], F32, name="c_rows")
+        nc.vector.tensor_copy(c_rows[:], c_bank[:])
 
         windows = []
         for b in range(BLOCKS):

@@ -7,6 +7,7 @@ P = 128
 S = 512
 M = 512
 N = 384
+G = 32
 BLOCKS = M // P
 WARM_MATMULS = 3
 
@@ -20,8 +21,9 @@ def tile_scatter_matmul_kernel(tc, base, x, w, c, offs, out):
         tc.tile_pool(name="held", bufs=1) as held,
         tc.psum_pool(name="banks", bufs=1) as banks,
     ):
-        c_row = held.tile([1, S], F32, name="c_row")
-        nc.scalar.dma_start(c_row[:], c)
+        c_seeds = held.tile([P, S], F32, name="c_seeds", align_bytes=64)
+        nc.gpsimd.memset(c_seeds[:], 0.0)
+        nc.scalar.dma_start(c_seeds[0:P:G, :], c.partition_broadcast(P // G))
 
         offsets = held.tile([P, N // 16], U16, name="offsets")
         nc.sync.dma_start(offsets[:], offs)
@@ -47,12 +49,15 @@ def tile_scatter_matmul_kernel(tc, base, x, w, c, offs, out):
         nc.vector.memset(ident[:], 0.0)
         make_identity(nc, ident[:], nomemset=True)
 
-        ones = held.tile([1, P], F32, name="ones")
-        nc.vector.memset(ones[:], 1.0)
-        c_bank = banks.tile([P, S], F32, name="c_bank")
-        nc.tensor.matmul(c_bank[:], ones[:], c_row[:], start=True, stop=True)
-        c_rows = held.tile([P, S], F32, name="c_rows")
-        nc.vector.tensor_copy(c_rows[:], c_bank[:])
+        c_turned = held.tile([P, S], F32, name="c_turned", align_bytes=64)
+        nc.vector.transpose(c_turned[:], c_seeds[:])
+        c_repeated = held.tile([P, S], F32, name="c_repeated", align_bytes=64)
+        nc.vector.tensor_copy(
+            c_repeated[:].rearrange("p (j a) -> p j a", a=G),
+            c_turned[:].rearrange("p (j a) -> p j a", a=G)[:, :, 0:1].to_broadcast([P, S // G, G]),
+        )
+        c_rows = held.tile([P, S], F32, name="c_rows", align_bytes=64)
+        nc.vector.transpose(c_rows[:], c_repeated[:])
 
         windows = []
         for b in range(BLOCKS):

@@ -21,9 +21,10 @@ def tile_scatter_matmul_kernel(tc, base, x, w, c, offs, out):
         tc.tile_pool(name="held", bufs=1) as held,
         tc.psum_pool(name="banks", bufs=1) as banks,
     ):
-        c_seeds = held.tile([P, S], F32, name="c_seeds", align_bytes=64)
+        c_seeds = held.tile([P, S // 2], F32, name="c_seeds", align_bytes=64)
         nc.gpsimd.memset(c_seeds[:], 0.0)
-        nc.scalar.dma_start(c_seeds[0:P:G, :], c.partition_broadcast(P // G))
+        nc.sync.dma_start(c_seeds[0:P:G, :], c[:, 0 : S // 2].partition_broadcast(P // G))
+        nc.scalar.dma_start(c_seeds[G // 2 : P : G, :], c[:, S // 2 : S].partition_broadcast(P // G))
 
         offsets = held.tile([P, N // 16], U16, name="offsets")
         nc.sync.dma_start(offsets[:], offs)
@@ -49,12 +50,14 @@ def tile_scatter_matmul_kernel(tc, base, x, w, c, offs, out):
         nc.vector.memset(ident[:], 0.0)
         make_identity(nc, ident[:], nomemset=True)
 
-        c_turned = held.tile([P, S], F32, name="c_turned", align_bytes=64)
+        c_turned = held.tile([P, S // 2], F32, name="c_turned", align_bytes=64)
         nc.vector.transpose(c_turned[:], c_seeds[:])
         c_repeated = held.tile([P, S], F32, name="c_repeated", align_bytes=64)
         nc.vector.tensor_copy(
-            c_repeated[:].rearrange("p (j a) -> p j a", a=G),
-            c_turned[:].rearrange("p (j a) -> p j a", a=G)[:, :, 0:1].to_broadcast([P, S // G, G]),
+            c_repeated[:].rearrange("p (h b a) -> p h b a", h=2, a=G),
+            c_turned[:]
+            .rearrange("p (b h e) -> p h b e", h=2, e=G // 2)[:, :, :, 0:1]
+            .to_broadcast([P, 2, S // (2 * G), G]),
         )
         c_rows = held.tile([P, S], F32, name="c_rows", align_bytes=64)
         nc.vector.transpose(c_rows[:], c_repeated[:])

@@ -29,14 +29,15 @@ def tile_scatter_matmul_kernel(tc, base, x, w, c, offs, out):
         offsets = held.tile([P, N // 16], U16, name="offsets")
         nc.sync.dma_start(offsets[:], offs)
 
-        base_blocks = []
-        for b in range(BLOCKS):
-            base_block = held.tile([P, S], BF16, name=f"base{b}")
-            queue = nc.sync if b % 2 == 0 else nc.scalar
-            queue.dma_start(base_block[:], base[b * P : (b + 1) * P, :])
-            base_blocks.append(base_block)
+        base_tile = held.tile([P, BLOCKS, S], BF16, name="base_tile")
+        nc.sync.dma_start(base_tile[:, 0, :], base[0:P, :])
+        nc.scalar.dma_start(base_tile[:, 1, :], base[P : 2 * P, :])
+        nc.sync.dma_start(
+            base_tile[:, 2:BLOCKS, :], base[2 * P : M, :].rearrange("(b p) s -> p b s", p=P)
+        )
+        base_blocks = [base_tile[:, b, :] for b in range(BLOCKS)]
         x_tile = held.tile([P, N], BF16, name="x_tile")
-        nc.sync.dma_start(x_tile[:], x)
+        nc.scalar.dma_start(x_tile[:], x)
         w_tile = held.tile([P, M], BF16, name="w_tile")
         nc.scalar.dma_start(w_tile[:], w)
 
@@ -65,7 +66,7 @@ def tile_scatter_matmul_kernel(tc, base, x, w, c, offs, out):
         windows = []
         for b in range(BLOCKS):
             window = banks.tile([P, S], F32, name=f"window{b}")
-            nc.tensor.matmul(window[:], ident[:], base_blocks[b][:], start=True, stop=True)
+            nc.tensor.matmul(window[:], ident[:], base_blocks[b], start=True, stop=True)
             windows.append(window)
 
         for b in range(BLOCKS):

@@ -26,20 +26,19 @@ def tile_scatter_matmul_kernel(tc, base, x, w, c, offs, out):
         nc.sync.dma_start(c_seeds[0:P:G, :], c[:, 0 : S // 2].partition_broadcast(P // G))
         nc.scalar.dma_start(c_seeds[G // 2 : P : G, :], c[:, S // 2 : S].partition_broadcast(P // G))
 
-        offsets = held.tile([P, N // 16], U16, name="offsets")
-        nc.sync.dma_start(offsets[:], offs)
-
         base_tile = held.tile([P, BLOCKS, S], BF16, name="base_tile")
         nc.sync.dma_start(base_tile[:, 0, :], base[0:P, :])
-        nc.scalar.dma_start(base_tile[:, 1, :], base[P : 2 * P, :])
+        nc.sync.dma_start(base_tile[:, 1, :], base[P : 2 * P, :])
         nc.sync.dma_start(
             base_tile[:, 2:BLOCKS, :], base[2 * P : M, :].rearrange("(b p) s -> p b s", p=P)
         )
         base_blocks = [base_tile[:, b, :] for b in range(BLOCKS)]
+        offsets = held.tile([P, N // 16], U16, name="offsets")
+        nc.sync.dma_start(offsets[:], offs)
         x_tile = held.tile([P, N], BF16, name="x_tile")
-        nc.scalar.dma_start(x_tile[:], x)
+        nc.sync.dma_start(x_tile[:], x)
         w_tile = held.tile([P, M], BF16, name="w_tile")
-        nc.scalar.dma_start(w_tile[:], w)
+        nc.sync.dma_start(w_tile[:], w)
 
         zeros = held.tile([P, S], BF16, name="zeros")
         nc.vector.memset(zeros[:], 0.0)
@@ -79,7 +78,13 @@ def tile_scatter_matmul_kernel(tc, base, x, w, c, offs, out):
             )
 
         for b in range(BLOCKS):
-            scaled = held.tile([P, S], F32, name=f"scaled{b}")
-            nc.vector.tensor_tensor(scaled[:], windows[b][:], c_rows[:], mybir.AluOpType.mult)
-            queue = nc.sync if b % 2 == 0 else nc.scalar
-            queue.dma_start(out[b * P : (b + 1) * P, :], scaled[:])
+            pieces = 2 if b == BLOCKS - 1 else 1
+            width = S // pieces
+            for piece in range(pieces):
+                columns = slice(piece * width, (piece + 1) * width)
+                scaled = held.tile([P, width], F32, name=f"scaled{b}_{piece}")
+                nc.vector.tensor_tensor(
+                    scaled[:], windows[b][:, columns], c_rows[:, columns], mybir.AluOpType.mult
+                )
+                queue = nc.sync if (b + piece) % 2 == 0 else nc.scalar
+                queue.dma_start(out[b * P : (b + 1) * P, columns], scaled[:])

@@ -37,8 +37,11 @@ def tile_scatter_matmul_kernel(tc, base, x, w, c, offs, out):
         nc.sync.dma_start(offsets[:], offs)
         x_tile = held.tile([P, N], BF16, name="x_tile")
         nc.sync.dma_start(x_tile[:], x)
-        w_tile = held.tile([P, M], BF16, name="w_tile")
-        nc.sync.dma_start(w_tile[:], w)
+        w_first = held.tile([P, P], BF16, name="w_first")
+        nc.sync.dma_start(w_first[:], w[:, 0:P])
+        w_rest = held.tile([P, M - P], BF16, name="w_rest")
+        nc.sync.dma_start(w_rest[:], w[:, P:M])
+        w_blocks = [w_first[:]] + [w_rest[:, (b - 1) * P : b * P] for b in range(1, BLOCKS)]
 
         zeros = held.tile([P, S], BF16, name="zeros")
         nc.vector.memset(zeros[:], 0.0)
@@ -71,7 +74,7 @@ def tile_scatter_matmul_kernel(tc, base, x, w, c, offs, out):
         for b in range(BLOCKS):
             nc.tensor.matmul(
                 windows[b][:].indirect(offsets[:]),
-                w_tile[:, b * P : (b + 1) * P],
+                w_blocks[b],
                 x_tile[:],
                 start=True,
                 stop=True,

@@ -26,13 +26,11 @@ def tile_scatter_matmul_kernel(tc, base, x, w, c, offs, out):
         nc.sync.dma_start(c_seeds[0:P:G, :], c[:, 0 : S // 2].partition_broadcast(P // G))
         nc.scalar.dma_start(c_seeds[G // 2 : P : G, :], c[:, S // 2 : S].partition_broadcast(P // G))
 
-        base_tile = held.tile([P, BLOCKS, S], BF16, name="base_tile")
-        nc.sync.dma_start(base_tile[:, 0, :], base[0:P, :])
-        nc.sync.dma_start(base_tile[:, 1, :], base[P : 2 * P, :])
-        nc.sync.dma_start(
-            base_tile[:, 2:BLOCKS, :], base[2 * P : M, :].rearrange("(b p) s -> p b s", p=P)
-        )
-        base_blocks = [base_tile[:, b, :] for b in range(BLOCKS)]
+        base_blocks = []
+        for b in range(BLOCKS):
+            base_block = held.tile([P, S], BF16, name=f"base_block{b}")
+            nc.sync.dma_start(base_block[:], base[b * P : (b + 1) * P, :])
+            base_blocks.append(base_block[:])
         offsets = held.tile([P, N // 16], U16, name="offsets")
         nc.sync.dma_start(offsets[:], offs)
         x_tile = held.tile([P, N], BF16, name="x_tile")

@@ -9,6 +9,7 @@ M = 512
 N = 384
 G = 32
 BLOCKS = M // P
+RUN_GAP = 24
 WARM_MATMULS = 3
 
 FLOPS = 2 * P * M * N
@@ -26,17 +27,16 @@ def tile_scatter_matmul_kernel(tc, base, x, w, c, offs, out):
         nc.sync.dma_start(c_seeds[0:P:G, :], c[:, 0 : S // 2].partition_broadcast(P // G))
         nc.scalar.dma_start(c_seeds[G // 2 : P : G, :], c[:, S // 2 : S].partition_broadcast(P // G))
 
-        base_blocks = []
-        for b in range(BLOCKS):
-            base_block = held.tile([P, S], BF16, name=f"base_block{b}")
-            nc.sync.dma_start(base_block[:], base[b * P : (b + 1) * P, :])
-            base_blocks.append(base_block[:])
+        base_blocks = [held.tile([P, S], BF16, name=f"base_block{b}") for b in range(BLOCKS)]
+        nc.sync.dma_start(base_blocks[0][:], base[0:P, :])
         offsets = held.tile([P, N // 16], U16, name="offsets")
         nc.sync.dma_start(offsets[:], offs)
         x_tile = held.tile([P, N], BF16, name="x_tile")
         nc.sync.dma_start(x_tile[:], x)
         w_first = held.tile([P, P], BF16, name="w_first")
         nc.sync.dma_start(w_first[:], w[:, 0:P])
+        for b in range(1, BLOCKS):
+            nc.sync.dma_start(base_blocks[b][:], base[b * P : (b + 1) * P, :])
         w_rest = held.tile([P, M - P], BF16, name="w_rest")
         nc.sync.dma_start(w_rest[:], w[:, P:M])
         w_blocks = [w_first[:]] + [w_rest[:, (b - 1) * P : b * P] for b in range(1, BLOCKS)]
@@ -63,20 +63,27 @@ def tile_scatter_matmul_kernel(tc, base, x, w, c, offs, out):
         c_rows = held.tile([P, S], F32, name="c_rows", align_bytes=64)
         nc.vector.transpose(c_rows[:], c_repeated[:])
 
-        windows = []
-        for b in range(BLOCKS):
-            window = banks.tile([P, S], F32, name=f"window{b}")
-            nc.tensor.matmul(window[:], ident[:], base_blocks[b], start=True, stop=True)
-            windows.append(window)
+        windows = [banks.tile([P, S], F32, name=f"window{b}") for b in range(BLOCKS)]
 
-        for b in range(BLOCKS):
+        def fill(b, pieces):
+            width = S // pieces
+            for piece in range(pieces):
+                columns = slice(piece * width, (piece + 1) * width)
+                nc.tensor.matmul(
+                    windows[b][:, columns], ident[:], base_blocks[b][:, columns], start=True, stop=True
+                )
+
+        def scatter(b):
             nc.tensor.matmul(
-                windows[b][:].indirect(offsets[:]),
-                w_blocks[b],
-                x_tile[:],
-                start=True,
-                stop=True,
+                windows[b][:].indirect(offsets[:]), w_blocks[b], x_tile[:], start=True, stop=True
             )
+
+        fill(0, 1)
+        scatter(0)
+        for b in range(1, BLOCKS):
+            fill(b, RUN_GAP // (BLOCKS - 1))
+        for b in range(1, BLOCKS):
+            scatter(b)
 
         for b in range(BLOCKS):
             pieces = 2 if b == BLOCKS - 1 else 1

import concourse.mybir as mybir
from concourse.masks import make_identity

BF16, F32, U16 = mybir.dt.bfloat16, mybir.dt.float32, mybir.dt.uint16

P = 128
S = 512
M = 512
N = 384
G = 32
BLOCKS = M // P
RUN_GAP = 24
WARM_MATMULS = 3

FLOPS = 2 * P * M * N
BYTES = P * N * 2 + P * M * 2 + S * 4 + P * (N // 16) * 2 + M * (S - N) * 2 + M * S * 4


def tile_scatter_matmul_kernel(tc, base, x, w, c, offs, out):
    nc = tc.nc
    with (
        tc.tile_pool(name="held", bufs=1) as held,
        tc.psum_pool(name="banks", bufs=1) as banks,
    ):
        c_seeds = held.tile([P, S // 2], F32, name="c_seeds", align_bytes=64)
        nc.gpsimd.memset(c_seeds[:], 0.0)
        nc.sync.dma_start(c_seeds[0:P:G, :], c[:, 0 : S // 2].partition_broadcast(P // G))
        nc.scalar.dma_start(c_seeds[G // 2 : P : G, :], c[:, S // 2 : S].partition_broadcast(P // G))

        base_blocks = [held.tile([P, S], BF16, name=f"base_block{b}") for b in range(BLOCKS)]
        nc.sync.dma_start(base_blocks[0][:], base[0:P, :])
        offsets = held.tile([P, N // 16], U16, name="offsets")
        nc.sync.dma_start(offsets[:], offs)
        x_tile = held.tile([P, N], BF16, name="x_tile")
        nc.sync.dma_start(x_tile[:], x)
        w_first = held.tile([P, P], BF16, name="w_first")
        nc.sync.dma_start(w_first[:], w[:, 0:P])
        for b in range(1, BLOCKS):
            nc.sync.dma_start(base_blocks[b][:], base[b * P : (b + 1) * P, :])
        w_rest = held.tile([P, M - P], BF16, name="w_rest")
        nc.sync.dma_start(w_rest[:], w[:, P:M])
        w_blocks = [w_first[:]] + [w_rest[:, (b - 1) * P : b * P] for b in range(1, BLOCKS)]

        zeros = held.tile([P, S], BF16, name="zeros")
        nc.vector.memset(zeros[:], 0.0)
        unread = banks.tile([P, S], F32, name="unread")
        for i in range(WARM_MATMULS):
            nc.tensor.matmul(unread[:], zeros[:, 0:P], zeros[:], start=True, stop=True)

        ident = held.tile([P, P], BF16, name="ident")
        nc.vector.memset(ident[:], 0.0)
        make_identity(nc, ident[:], nomemset=True)

        c_turned = held.tile([P, S // 2], F32, name="c_turned", align_bytes=64)
        nc.vector.transpose(c_turned[:], c_seeds[:])
        c_repeated = held.tile([P, S], F32, name="c_repeated", align_bytes=64)
        nc.vector.tensor_copy(
            c_repeated[:].rearrange("p (h b a) -> p h b a", h=2, a=G),
            c_turned[:]
            .rearrange("p (b h e) -> p h b e", h=2, e=G // 2)[:, :, :, 0:1]
            .to_broadcast([P, 2, S // (2 * G), G]),
        )
        c_rows = held.tile([P, S], F32, name="c_rows", align_bytes=64)
        nc.vector.transpose(c_rows[:], c_repeated[:])

        windows = [banks.tile([P, S], F32, name=f"window{b}") for b in range(BLOCKS)]

        def fill(b, pieces):
            width = S // pieces
            for piece in range(pieces):
                columns = slice(piece * width, (piece + 1) * width)
                nc.tensor.matmul(
                    windows[b][:, columns], ident[:], base_blocks[b][:, columns], start=True, stop=True
                )

        def scatter(b):
            nc.tensor.matmul(
                windows[b][:].indirect(offsets[:]), w_blocks[b], x_tile[:], start=True, stop=True
            )

        fill(0, 1)
        scatter(0)
        for b in range(1, BLOCKS):
            fill(b, RUN_GAP // (BLOCKS - 1))
        for b in range(1, BLOCKS):
            scatter(b)

        for b in range(BLOCKS):
            pieces = 2 if b == BLOCKS - 1 else 1
            width = S // pieces
            for piece in range(pieces):
                columns = slice(piece * width, (piece + 1) * width)
                scaled = held.tile([P, width], F32, name=f"scaled{b}_{piece}")
                nc.vector.tensor_tensor(
                    scaled[:], windows[b][:, columns], c_rows[:, columns], mybir.AluOpType.mult
                )
                queue = nc.sync if (b + piece) % 2 == 0 else nc.scalar
                queue.dma_start(out[b * P : (b + 1) * P, columns], scaled[:])
